import numpy as np
import ml_dtypes


def mxq(x, axis, fmt="e4m3"):
    dtype, down = {"e4m3": (ml_dtypes.float8_e4m3fn, 7), "e5m2": (ml_dtypes.float8_e5m2, 14)}[fmt]
    v = np.moveaxis(np.asarray(x, np.float32).astype(ml_dtypes.bfloat16).astype(np.float64), axis, -1)
    blocks = v.reshape(v.shape[:-1] + (-1, 32))
    amax = np.abs(blocks).max(-1, keepdims=True)
    byte = np.maximum(np.where(amax > 0, np.frexp(amax)[1] - 1 + 127, 0) - down, 1)
    scale = np.exp2(byte - 127.0)
    codes = (blocks / scale).astype(np.float32).astype(dtype).astype(np.float64)
    return np.moveaxis((codes * scale).reshape(v.shape), -1, axis)


WIDE = False


def mx_kscale(k):
    if not WIDE:
        return np.ones(k)
    levels = np.array([10, -10, 5, -5, 0])
    if k % 512:
        return np.exp2(np.random.permutation(np.resize(levels, k // 32))).repeat(32)
    a = np.empty((k // 512, 16))
    for p in range(k // 512):
        a[p, :8] = np.random.permutation(np.resize(levels, 8))
        for g in range(8):
            far = levels[np.abs(levels - a[p, g]) >= 10]
            a[p, g + 8] = far[np.random.randint(len(far))]
    return np.exp2(a.ravel()).repeat(32)


def f64(x):
    return np.asarray(x).astype(np.float64)


def striped(idx):
    return np.tile(np.asarray(idx).reshape(-1, 16).T, (8, 1)).astype(np.uint16)


def unstriped(offs):
    return offs[:16].T.reshape(-1).astype(np.int64)


E2M1 = np.array([0.0, 0.5, 1.0, 1.5, 2.0, 3.0, 4.0, 6.0, -0.0, -0.5, -1.0, -1.5, -2.0, -3.0, -4.0, -6.0])


def pack_weight(w, fmt):
    k, n = w.shape
    w = f64(np.asarray(w, np.float32).astype(ml_dtypes.bfloat16)).reshape(k // 32, 32, n)
    amax = np.abs(w).max(1)
    if fmt == "e4m3":
        byte = np.frexp(amax)[1] - 1 + 127 - 7
    else:
        mant, ex = np.frexp(amax / 6.0)
        byte = np.where(mant > 0.5, ex, ex - 1) + 127
    byte = np.clip(np.where(amax > 0, byte, 1), 1, 254)
    scaled = (w * np.exp2(127.0 - byte)[:, None, :]).reshape(k, n).astype(np.float32)
    by_word = np.ascontiguousarray(scaled.reshape(k // 512, 128, 4, n).transpose(0, 1, 3, 2))
    if fmt == "e4m3":
        words = by_word.astype(ml_dtypes.float8_e4m3fn).view(np.uint8)
    else:
        c = by_word.astype(ml_dtypes.float4_e2m1fn).view(np.uint8) & 0xF
        words = (c[..., 0::2] | (c[..., 1::2] << 4)).reshape(k // 512, 128, 2 * n)
    return np.ascontiguousarray(words), np.ascontiguousarray(byte.astype(np.uint8).reshape(k // 512, 16, n))


def unpack_weight(words, scales, fmt):
    g, _, n = scales.shape
    words = np.ascontiguousarray(words).reshape(g, 128, n, -1)
    if fmt == "e4m3":
        vals = words.view(ml_dtypes.float8_e4m3fn).astype(np.float64)
    else:
        nib = np.empty((g, 128, n, 4), np.uint8)
        nib[..., 0::2] = words & 0xF
        nib[..., 1::2] = words >> 4
        vals = E2M1[nib]
    vals = vals * np.repeat(np.exp2(scales.astype(np.float64) - 127.0), 8, axis=1)[..., None]
    return vals.transpose(0, 1, 3, 2).reshape(g * 512, n)


B, N, T, D, NQ = 1, 512, 4096, 512, 128


def setup_inputs():
    n = np.random.standard_normal
    idx = np.sort(np.random.permutation(T)[:B * N].reshape(B, N), axis=1).reshape(-1)
    s = mx_kscale(D)[:, None]
    kp = pack_weight(n((D, T)) / s, "e4m3")
    return {
        "qT": (n((B, D, NQ)) * s * (1.00 / np.sqrt(D))).astype(np.float32),
        "k_words": kp[0],
        "k_scales": kp[1],
        "ls": (np.random.uniform(8.5, 9.0, (B, NQ, 1))).astype(np.float32),
        "pd": (np.exp(0.7 * n((B, NQ, N)) - 8.8)).astype(np.float32),
        "offs": striped(idx),
    }


def reference(qT, k_words, k_scales, ls, pd, offs):
    idx = unstriped(offs)
    pick = lambda x, which: x[:, which].reshape(x.shape[0], B, -1).transpose(1, 0, 2)
    k = unpack_weight(k_words, k_scales, "e4m3")
    kg = pick(k, idx)
    qq = mxq(f64(qT), 1, "e4m3")
    a = qq.transpose(0, 2, 1) @ kg
    y = np.minimum(np.exp(a - f64(ls)) / f64(pd), 1.0)
    return y

@@ -1,0 +1,93 @@
+import math
+from contextlib import ExitStack
+
+import concourse.mybir as mybir
+
+F32 = mybir.dt.float32
+BF16 = mybir.dt.bfloat16
+I32 = mybir.dt.int32
+U32 = mybir.dt.uint32
+U16 = mybir.dt.uint16
+U8 = mybir.dt.uint8
+FP8X4 = mybir.dt.float8_e4m3fn_x4
+ALU = mybir.AluOpType
+ACT = mybir.ActivationFunctionType
+
+P = 128
+PACK = 4
+D, T, N, NQ = 512, 4096, 512, 128
+CHUNKS = [128,128,128,128]
+LOG2_SHIFT = 62
+FLOPS = 2 * D * NQ * N
+
+
+def tile_attend_accept_srt_kernel(tc, qT, k_words, k_scales, ls, pd, offs, out):
+    nc = tc.nc
+    with ExitStack() as ctx:
+        sb = ctx.enter_context(tc.tile_pool(name="sb", bufs=1))
+        ps = ctx.enter_context(tc.psum_pool(name="ps", bufs=1))
+
+        offsets = sb.tile([P, N // 16], U16, name="offsets")
+        nc.sync.dma_start(offsets[:], offs)
+
+        scale_pool = sb.tile([P, T], U8, name="scale_pool", align_bytes=64)
+        nc.vector.memset(scale_pool[:].bitcast(I32), 0)
+        key_plane = sb.tile([P, N], U8, name="key_plane", align_bytes=64)
+        nc.vector.memset(key_plane[:].bitcast(I32), 0)
+
+        draft = sb.tile([P, N], F32, name="draft")
+        q_raw = sb.tile([P, PACK, NQ], F32, name="q_raw")
+        lse = sb.tile([P, 1], F32, name="lse")
+        word_pool = sb.tile([P, T], U32, name="word_pool", align_bytes=64)
+        nc.sync.dma_start(draft[:], pd[0])
+        nc.sync.dma_start(q_raw[:], qT[0].rearrange("(p j) w -> p j w", j=PACK))
+        nc.scalar.dma_start(scale_pool[0:P:8, :].bitcast(I32), k_scales[0].bitcast(I32))
+        nc.sync.dma_start(word_pool[:].bitcast(I32), k_words[0].rearrange("p n t -> p (n t)").bitcast(I32))
+        nc.sync.dma_start(lse[:], ls[0])
+
+        log_draft = sb.tile([P, N], F32, name="log_draft")
+
+        nc.scalar.activation(log_draft[:], draft[:], ACT.Ln, scale=2.0**LOG2_SHIFT)
+
+        q_bf = sb.tile([P, NQ, PACK], BF16, name="q_bf", align_bytes=64)
+        nc.vector.tensor_copy(q_bf[:], q_raw[:].rearrange("p j w -> p w j"))
+        listed_scales = sb.tile([P, N], U8, name="listed_scales", align_bytes=64)
+        nc.vector.tensor_copy(listed_scales[:], scale_pool[:].indirect(offsets[:]))
+        q_words = sb.tile([P, NQ], U32, name="q_words", align_bytes=64)
+        q_plane = sb.tile([P, NQ], U8, name="q_plane", align_bytes=64)
+        nc.vector.quantize_mx(
+            out=q_words[:].bitcast(FP8X4),
+            scales=q_plane[:],
+            in_=q_bf[:].rearrange("p w j -> p (w j)"),
+        )
+        for r in range(4):
+            nc.scalar.dma_start(key_plane[r:P:32, :].bitcast(I32), listed_scales[8 * r : P : 32, :].bitcast(I32))
+
+        key_words = sb.tile([P, N], U32, name="key_words", align_bytes=64)
+        nc.vector.tensor_copy(key_words[:], word_pool[:].indirect(offsets[:]))
+
+        c0 = 0
+        for i, width in enumerate(CHUNKS):
+            cols = slice(c0, c0 + width)
+            c0 += width
+            acc = ps.tile([P, width], F32, name="acc%d" % i)
+            nc.tensor.matmul_mx(
+                out=acc[:],
+                lhsT=q_words[:].bitcast(FP8X4),
+                lhsT_scale=q_plane[:],
+                rhs=key_words[:, cols].bitcast(FP8X4),
+                rhs_scale=key_plane[:, cols],
+                start=True,
+                stop=True,
+            )
+            gap = sb.tile([P, width], F32, name="gap%d" % i)
+            nc.vector.scalar_tensor_tensor(
+                gap[:], acc[:], lse[:, 0:1], log_draft[:, cols], ALU.subtract, ALU.subtract
+            )
+            capped = sb.tile([P, width], F32, name="capped%d" % i)
+            nc.vector.tensor_scalar(
+                capped[:], gap[:], LOG2_SHIFT * math.log(2.0), 0.0, ALU.add, ALU.min
+            )
+            accept = sb.tile([P, width], F32, name="accept%d" % i)
+            nc.scalar.activation(accept[:], capped[:], ACT.Exp)
+            nc.sync.dma_start(out[0][:, cols], accept[:])

@@ -39,11 +39,11 @@ def tile_attend_accept_srt_kernel(tc, qT, k_words, k_scales, ls, pd, offs, out):
         q_raw = sb.tile([P, PACK, NQ], F32, name="q_raw")
         lse = sb.tile([P, 1], F32, name="lse")
         word_pool = sb.tile([P, T], U32, name="word_pool", align_bytes=64)
+        nc.scalar.dma_start(lse[:], ls[0])
         nc.sync.dma_start(draft[:], pd[0])
         nc.sync.dma_start(q_raw[:], qT[0].rearrange("(p j) w -> p j w", j=PACK))
-        nc.scalar.dma_start(scale_pool[0:P:8, :].bitcast(I32), k_scales[0].bitcast(I32))
+        nc.sync.dma_start(scale_pool[0:P:8, :].bitcast(I32), k_scales[0].bitcast(I32))
         nc.sync.dma_start(word_pool[:].bitcast(I32), k_words[0].rearrange("p n t -> p (n t)").bitcast(I32))
-        nc.sync.dma_start(lse[:], ls[0])
 
         log_draft = sb.tile([P, N], F32, name="log_draft")
 

@@ -28,7 +28,6 @@ def tile_attend_accept_srt_kernel(tc, qT, k_words, k_scales, ls, pd, offs, out):
         ps = ctx.enter_context(tc.psum_pool(name="ps", bufs=1))
 
         offsets = sb.tile([P, N // 16], U16, name="offsets")
-        nc.sync.dma_start(offsets[:], offs)
 
         scale_pool = sb.tile([P, T], U8, name="scale_pool", align_bytes=64)
         nc.vector.memset(scale_pool[:].bitcast(I32), 0)
@@ -39,11 +38,12 @@ def tile_attend_accept_srt_kernel(tc, qT, k_words, k_scales, ls, pd, offs, out):
         q_raw = sb.tile([P, PACK, NQ], F32, name="q_raw")
         lse = sb.tile([P, 1], F32, name="lse")
         word_pool = sb.tile([P, T], U32, name="word_pool", align_bytes=64)
-        nc.scalar.dma_start(lse[:], ls[0])
         nc.sync.dma_start(draft[:], pd[0])
+        nc.sync.dma_start(offsets[:], offs)
         nc.sync.dma_start(q_raw[:], qT[0].rearrange("(p j) w -> p j w", j=PACK))
         nc.sync.dma_start(scale_pool[0:P:8, :].bitcast(I32), k_scales[0].bitcast(I32))
         nc.sync.dma_start(word_pool[:].bitcast(I32), k_words[0].rearrange("p n t -> p (n t)").bitcast(I32))
+        nc.sync.dma_start(lse[:], ls[0])
 
         log_draft = sb.tile([P, N], F32, name="log_draft")
 
@@ -84,10 +84,8 @@ def tile_attend_accept_srt_kernel(tc, qT, k_words, k_scales, ls, pd, offs, out):
             nc.vector.scalar_tensor_tensor(
                 gap[:], acc[:], lse[:, 0:1], log_draft[:, cols], ALU.subtract, ALU.subtract
             )
-            capped = sb.tile([P, width], F32, name="capped%d" % i)
-            nc.vector.tensor_scalar(
-                capped[:], gap[:], LOG2_SHIFT * math.log(2.0), 0.0, ALU.add, ALU.min
-            )
+            ratio = sb.tile([P, width], F32, name="ratio%d" % i)
+            nc.scalar.activation(ratio[:], gap[:], ACT.Exp, bias=LOG2_SHIFT * math.log(2.0))
             accept = sb.tile([P, width], F32, name="accept%d" % i)
-            nc.scalar.activation(accept[:], capped[:], ACT.Exp)
+            nc.vector.tensor_scalar_min(accept[:], ratio[:], 1.0)
             nc.sync.dma_start(out[0][:, cols], accept[:])

@@ -36,20 +36,18 @@ def tile_attend_accept_srt_kernel(tc, qT, k_words, k_scales, ls, pd, offs, out):
 
         draft = sb.tile([P, N], F32, name="draft")
         q_raw = sb.tile([P, PACK, NQ], F32, name="q_raw")
-        lse = sb.tile([P, 1], F32, name="lse")
         word_pool = sb.tile([P, T], U32, name="word_pool", align_bytes=64)
         nc.sync.dma_start(draft[:], pd[0])
         nc.sync.dma_start(offsets[:], offs)
         nc.sync.dma_start(q_raw[:], qT[0].rearrange("(p j) w -> p j w", j=PACK))
         nc.sync.dma_start(scale_pool[0:P:8, :].bitcast(I32), k_scales[0].bitcast(I32))
         nc.sync.dma_start(word_pool[:].bitcast(I32), k_words[0].rearrange("p n t -> p (n t)").bitcast(I32))
-        nc.sync.dma_start(lse[:], ls[0])
 
         log_draft = sb.tile([P, N], F32, name="log_draft")
 
         nc.scalar.activation(log_draft[:], draft[:], ACT.Ln, scale=2.0**LOG2_SHIFT)
 
-        q_bf = sb.tile([P, NQ, PACK], BF16, name="q_bf", align_bytes=64)
+        q_bf = sb.tile([P, NQ, PACK], BF16, name="q_bf", tag="q_bf", align_bytes=64)
         nc.vector.tensor_copy(q_bf[:], q_raw[:].rearrange("p j w -> p w j"))
         listed_scales = sb.tile([P, N], U8, name="listed_scales", align_bytes=64)
         nc.vector.tensor_copy(listed_scales[:], scale_pool[:].indirect(offsets[:]))
@@ -61,7 +59,9 @@ def tile_attend_accept_srt_kernel(tc, qT, k_words, k_scales, ls, pd, offs, out):
             in_=q_bf[:].rearrange("p w j -> p (w j)"),
         )
         for r in range(4):
-            nc.scalar.dma_start(key_plane[r:P:32, :].bitcast(I32), listed_scales[8 * r : P : 32, :].bitcast(I32))
+            nc.sync.dma_start(key_plane[r:P:32, :].bitcast(I32), listed_scales[8 * r : P : 32, :].bitcast(I32))
+        lse = sb.tile([P, 1], F32, name="lse", tag="q_bf", align_bytes=64)
+        nc.sync.dma_start(lse[:], ls[0])
 
         key_words = sb.tile([P, N], U32, name="key_words", align_bytes=64)
         nc.vector.tensor_copy(key_words[:], word_pool[:].indirect(offsets[:]))

@@ -17,6 +17,7 @@ P = 128
 PACK = 4
 D, T, N, NQ = 512, 4096, 512, 128
 CHUNKS = [128,128,128,128]
+EARLY = 256
 LOG2_SHIFT = 62
 FLOPS = 2 * D * NQ * N
 
@@ -34,18 +35,21 @@ def tile_attend_accept_srt_kernel(tc, qT, k_words, k_scales, ls, pd, offs, out):
         key_plane = sb.tile([P, N], U8, name="key_plane", align_bytes=64)
         nc.vector.memset(key_plane[:].bitcast(I32), 0)
 
-        draft = sb.tile([P, N], F32, name="draft")
+        draft_early = sb.tile([P, EARLY], F32, name="draft_early")
+        draft_late = sb.tile([P, N - EARLY], F32, name="draft_late")
         q_raw = sb.tile([P, PACK, NQ], F32, name="q_raw")
         word_pool = sb.tile([P, T], U32, name="word_pool", align_bytes=64)
-        nc.sync.dma_start(draft[:], pd[0])
+        nc.sync.dma_start(draft_early[:], pd[0][:, :EARLY])
         nc.sync.dma_start(offsets[:], offs)
         nc.sync.dma_start(q_raw[:], qT[0].rearrange("(p j) w -> p j w", j=PACK))
         nc.sync.dma_start(scale_pool[0:P:8, :].bitcast(I32), k_scales[0].bitcast(I32))
         nc.sync.dma_start(word_pool[:].bitcast(I32), k_words[0].rearrange("p n t -> p (n t)").bitcast(I32))
+        nc.sync.dma_start(draft_late[:], pd[0][:, EARLY:])
 
         log_draft = sb.tile([P, N], F32, name="log_draft")
 
-        nc.scalar.activation(log_draft[:], draft[:], ACT.Ln, scale=2.0**LOG2_SHIFT)
+        nc.scalar.activation(log_draft[:, :EARLY], draft_early[:], ACT.Ln, scale=2.0**LOG2_SHIFT)
+        nc.scalar.activation(log_draft[:, EARLY:], draft_late[:], ACT.Ln, scale=2.0**LOG2_SHIFT)
 
         q_bf = sb.tile([P, NQ, PACK], BF16, name="q_bf", tag="q_bf", align_bytes=64)
         nc.vector.tensor_copy(q_bf[:], q_raw[:].rearrange("p j w -> p w j"))

@@ -18,6 +18,7 @@ PACK = 4
 D, T, N, NQ = 512, 4096, 512, 128
 CHUNKS = [128,128,128,128]
 EARLY = 256
+ROW0, ROW_STEP = 11, 7
 LOG2_SHIFT = 62
 FLOPS = 2 * D * NQ * N
 
@@ -42,7 +43,7 @@ def tile_attend_accept_srt_kernel(tc, qT, k_words, k_scales, ls, pd, offs, out):
         nc.sync.dma_start(draft_early[:], pd[0][:, :EARLY])
         nc.sync.dma_start(offsets[:], offs)
         nc.sync.dma_start(q_raw[:], qT[0].rearrange("(p j) w -> p j w", j=PACK))
-        nc.sync.dma_start(scale_pool[0:P:8, :].bitcast(I32), k_scales[0].bitcast(I32))
+        nc.sync.dma_start(scale_pool[ROW0 : ROW0 + 16 * ROW_STEP : ROW_STEP, :].bitcast(I32), k_scales[0].bitcast(I32))
         nc.sync.dma_start(word_pool[:].bitcast(I32), k_words[0].rearrange("p n t -> p (n t)").bitcast(I32))
         nc.sync.dma_start(draft_late[:], pd[0][:, EARLY:])
 
@@ -63,14 +64,16 @@ def tile_attend_accept_srt_kernel(tc, qT, k_words, k_scales, ls, pd, offs, out):
             in_=q_bf[:].rearrange("p w j -> p (w j)"),
         )
         for r in range(4):
-            nc.sync.dma_start(key_plane[r:P:32, :].bitcast(I32), listed_scales[8 * r : P : 32, :].bitcast(I32))
+            nc.sync.dma_start(key_plane[r:P:32, :].bitcast(I32), listed_scales[ROW0 + ROW_STEP * r : ROW0 + 16 * ROW_STEP : 4 * ROW_STEP, :].bitcast(I32))
         lse = sb.tile([P, 1], F32, name="lse", tag="q_bf", align_bytes=64)
         nc.sync.dma_start(lse[:], ls[0])
 
         key_words = sb.tile([P, N], U32, name="key_words", align_bytes=64)
         nc.vector.tensor_copy(key_words[:], word_pool[:].indirect(offsets[:]))
 
+        accept = sb.tile([P, N], F32, name="accept")
         c0 = 0
+        stored = 0
         for i, width in enumerate(CHUNKS):
             cols = slice(c0, c0 + width)
             c0 += width
@@ -90,6 +93,7 @@ def tile_attend_accept_srt_kernel(tc, qT, k_words, k_scales, ls, pd, offs, out):
             )
             ratio = sb.tile([P, width], F32, name="ratio%d" % i)
             nc.scalar.activation(ratio[:], gap[:], ACT.Exp, bias=LOG2_SHIFT * math.log(2.0))
-            accept = sb.tile([P, width], F32, name="accept%d" % i)
-            nc.vector.tensor_scalar_min(accept[:], ratio[:], 1.0)
-            nc.sync.dma_start(out[0][:, cols], accept[:])
+            nc.vector.tensor_scalar_min(accept[:, cols], ratio[:], 1.0)
+            if i != len(CHUNKS) - 2:
+                nc.sync.dma_start(out[0][:, stored:c0], accept[:, stored:c0])
+                stored = c0

@@ -18,7 +18,7 @@ PACK = 4
 D, T, N, NQ = 512, 4096, 512, 128
 CHUNKS = [128,128,128,128]
 EARLY = 256
-ROW0, ROW_STEP = 11, 7
+ROW0, ROW_STEP = 32, 4
 LOG2_SHIFT = 62
 FLOPS = 2 * D * NQ * N
 

@@ -17,7 +17,7 @@ P = 128
 PACK = 4
 D, T, N, NQ = 512, 4096, 512, 128
 CHUNKS = [128,128,128,128]
-EARLY = 256
+DRAFT_PIECES = [(0, 128), (128, 384), (384, 512)]
 ROW0, ROW_STEP = 32, 4
 LOG2_SHIFT = 62
 FLOPS = 2 * D * NQ * N
@@ -36,21 +36,21 @@ def tile_attend_accept_srt_kernel(tc, qT, k_words, k_scales, ls, pd, offs, out):
         key_plane = sb.tile([P, N], U8, name="key_plane", align_bytes=64)
         nc.vector.memset(key_plane[:].bitcast(I32), 0)
 
-        draft_early = sb.tile([P, EARLY], F32, name="draft_early")
-        draft_late = sb.tile([P, N - EARLY], F32, name="draft_late")
+        drafts = [sb.tile([P, b - a], F32, name="draft%d" % a) for a, b in DRAFT_PIECES]
         q_raw = sb.tile([P, PACK, NQ], F32, name="q_raw")
         word_pool = sb.tile([P, T], U32, name="word_pool", align_bytes=64)
-        nc.sync.dma_start(draft_early[:], pd[0][:, :EARLY])
+        nc.sync.dma_start(drafts[0][:], pd[0][:, slice(*DRAFT_PIECES[0])])
         nc.sync.dma_start(offsets[:], offs)
         nc.sync.dma_start(q_raw[:], qT[0].rearrange("(p j) w -> p j w", j=PACK))
         nc.sync.dma_start(scale_pool[ROW0 : ROW0 + 16 * ROW_STEP : ROW_STEP, :].bitcast(I32), k_scales[0].bitcast(I32))
         nc.sync.dma_start(word_pool[:].bitcast(I32), k_words[0].rearrange("p n t -> p (n t)").bitcast(I32))
-        nc.sync.dma_start(draft_late[:], pd[0][:, EARLY:])
+        for draft, (a, b) in zip(drafts[1:], DRAFT_PIECES[1:]):
+            nc.sync.dma_start(draft[:], pd[0][:, a:b])
 
         log_draft = sb.tile([P, N], F32, name="log_draft")
 
-        nc.scalar.activation(log_draft[:, :EARLY], draft_early[:], ACT.Ln, scale=2.0**LOG2_SHIFT)
-        nc.scalar.activation(log_draft[:, EARLY:], draft_late[:], ACT.Ln, scale=2.0**LOG2_SHIFT)
+        for draft, (a, b) in zip(drafts, DRAFT_PIECES):
+            nc.scalar.activation(log_draft[:, a:b], draft[:], ACT.Ln, scale=2.0**LOG2_SHIFT)
 
         q_bf = sb.tile([P, NQ, PACK], BF16, name="q_bf", tag="q_bf", align_bytes=64)
         nc.vector.tensor_copy(q_bf[:], q_raw[:].rearrange("p j w -> p w j"))
@@ -64,7 +64,7 @@ def tile_attend_accept_srt_kernel(tc, qT, k_words, k_scales, ls, pd, offs, out):
             in_=q_bf[:].rearrange("p w j -> p (w j)"),
         )
         for r in range(4):
-            nc.sync.dma_start(key_plane[r:P:32, :].bitcast(I32), listed_scales[ROW0 + ROW_STEP * r : ROW0 + 16 * ROW_STEP : 4 * ROW_STEP, :].bitcast(I32))
+            nc.scalar.dma_start(key_plane[r:P:32, :].bitcast(I32), listed_scales[ROW0 + ROW_STEP * r : ROW0 + 16 * ROW_STEP : 4 * ROW_STEP, :].bitcast(I32))
         lse = sb.tile([P, 1], F32, name="lse", tag="q_bf", align_bytes=64)
         nc.sync.dma_start(lse[:], ls[0])
 

@@ -39,9 +39,9 @@ def tile_attend_accept_srt_kernel(tc, qT, k_words, k_scales, ls, pd, offs, out):
         drafts = [sb.tile([P, b - a], F32, name="draft%d" % a) for a, b in DRAFT_PIECES]
         q_raw = sb.tile([P, PACK, NQ], F32, name="q_raw")
         word_pool = sb.tile([P, T], U32, name="word_pool", align_bytes=64)
-        nc.sync.dma_start(drafts[0][:], pd[0][:, slice(*DRAFT_PIECES[0])])
-        nc.sync.dma_start(offsets[:], offs)
         nc.sync.dma_start(q_raw[:], qT[0].rearrange("(p j) w -> p j w", j=PACK))
+        nc.sync.dma_start(offsets[:], offs)
+        nc.sync.dma_start(drafts[0][:], pd[0][:, slice(*DRAFT_PIECES[0])])
         nc.sync.dma_start(scale_pool[ROW0 : ROW0 + 16 * ROW_STEP : ROW_STEP, :].bitcast(I32), k_scales[0].bitcast(I32))
         nc.sync.dma_start(word_pool[:].bitcast(I32), k_words[0].rearrange("p n t -> p (n t)").bitcast(I32))
         for draft, (a, b) in zip(drafts[1:], DRAFT_PIECES[1:]):

@@ -1,4 +1,3 @@
-import math
 from contextlib import ExitStack
 
 import concourse.mybir as mybir
@@ -17,8 +16,9 @@ P = 128
 PACK = 4
 D, T, N, NQ = 512, 4096, 512, 128
 CHUNKS = [128,128,128,128]
-DRAFT_PIECES = [(0, 128), (128, 384), (384, 512)]
+DRAFT_PIECES = [(0, 256), (256, 512)]
 ROW0, ROW_STEP = 32, 4
+FIRST = 256
 LOG2_SHIFT = 62
 FLOPS = 2 * D * NQ * N
 
@@ -41,12 +41,17 @@ def tile_attend_accept_srt_kernel(tc, qT, k_words, k_scales, ls, pd, offs, out):
         word_pool = sb.tile([P, T], U32, name="word_pool", align_bytes=64)
         nc.sync.dma_start(q_raw[:], qT[0].rearrange("(p j) w -> p j w", j=PACK))
         nc.sync.dma_start(offsets[:], offs)
-        nc.sync.dma_start(drafts[0][:], pd[0][:, slice(*DRAFT_PIECES[0])])
+        words_hbm = k_words[0].rearrange("p n t -> p (n t)").bitcast(I32)
+        nc.sync.dma_start(word_pool[:, :FIRST].bitcast(I32), words_hbm[:, :FIRST])
         nc.sync.dma_start(scale_pool[ROW0 : ROW0 + 16 * ROW_STEP : ROW_STEP, :].bitcast(I32), k_scales[0].bitcast(I32))
-        nc.sync.dma_start(word_pool[:].bitcast(I32), k_words[0].rearrange("p n t -> p (n t)").bitcast(I32))
-        for draft, (a, b) in zip(drafts[1:], DRAFT_PIECES[1:]):
+        nc.sync.dma_start(word_pool[:, FIRST:].bitcast(I32), words_hbm[:, FIRST:])
+        for draft, (a, b) in zip(drafts, DRAFT_PIECES):
             nc.sync.dma_start(draft[:], pd[0][:, a:b])
 
+        one = sb.tile([P, 1], F32, name="one")
+        nc.vector.memset(one[:], 1.0)
+        log_shift = sb.tile([P, 1], F32, name="log_shift")
+        nc.scalar.activation(log_shift[:], one[:], ACT.Ln, scale=2.0**LOG2_SHIFT)
         log_draft = sb.tile([P, N], F32, name="log_draft")
 
         for draft, (a, b) in zip(drafts, DRAFT_PIECES):
@@ -92,7 +97,7 @@ def tile_attend_accept_srt_kernel(tc, qT, k_words, k_scales, ls, pd, offs, out):
                 gap[:], acc[:], lse[:, 0:1], log_draft[:, cols], ALU.subtract, ALU.subtract
             )
             ratio = sb.tile([P, width], F32, name="ratio%d" % i)
-            nc.scalar.activation(ratio[:], gap[:], ACT.Exp, bias=LOG2_SHIFT * math.log(2.0))
+            nc.scalar.activation(ratio[:], gap[:], ACT.Exp, bias=log_shift[:, 0:1])
             nc.vector.tensor_scalar_min(accept[:, cols], ratio[:], 1.0)
             if i != len(CHUNKS) - 2:
                 nc.sync.dma_start(out[0][:, stored:c0], accept[:, stored:c0])

@@ -19,6 +19,7 @@ CHUNKS = [128,128,128,128]
 DRAFT_PIECES = [(0, 256), (256, 512)]
 ROW0, ROW_STEP = 32, 4
 FIRST = 256
+CAP_AFTER = 2
 LOG2_SHIFT = 62
 FLOPS = 2 * D * NQ * N
 
@@ -97,8 +98,12 @@ def tile_attend_accept_srt_kernel(tc, qT, k_words, k_scales, ls, pd, offs, out):
                 gap[:], acc[:], lse[:, 0:1], log_draft[:, cols], ALU.subtract, ALU.subtract
             )
             ratio = sb.tile([P, width], F32, name="ratio%d" % i)
-            nc.scalar.activation(ratio[:], gap[:], ACT.Exp, bias=log_shift[:, 0:1])
-            nc.vector.tensor_scalar_min(accept[:, cols], ratio[:], 1.0)
+            if i < CAP_AFTER:
+                nc.scalar.activation(ratio[:], gap[:], ACT.Exp, bias=log_shift[:, 0:1])
+                nc.vector.tensor_scalar_min(accept[:, cols], ratio[:], 1.0)
+            else:
+                nc.vector.tensor_scalar(ratio[:], gap[:], log_shift[:, 0:1], 0.0, ALU.add, ALU.min)
+                nc.scalar.activation(accept[:, cols], ratio[:], ACT.Exp)
             if i != len(CHUNKS) - 2:
                 nc.sync.dma_start(out[0][:, stored:c0], accept[:, stored:c0])
                 stored = c0

@@ -19,7 +19,6 @@ CHUNKS = [128,128,128,128]
 DRAFT_PIECES = [(0, 256), (256, 512)]
 ROW0, ROW_STEP = 32, 4
 FIRST = 256
-CAP_AFTER = 2
 LOG2_SHIFT = 62
 FLOPS = 2 * D * NQ * N
 
@@ -98,12 +97,8 @@ def tile_attend_accept_srt_kernel(tc, qT, k_words, k_scales, ls, pd, offs, out):
                 gap[:], acc[:], lse[:, 0:1], log_draft[:, cols], ALU.subtract, ALU.subtract
             )
             ratio = sb.tile([P, width], F32, name="ratio%d" % i)
-            if i < CAP_AFTER:
-                nc.scalar.activation(ratio[:], gap[:], ACT.Exp, bias=log_shift[:, 0:1])
-                nc.vector.tensor_scalar_min(accept[:, cols], ratio[:], 1.0)
-            else:
-                nc.vector.tensor_scalar(ratio[:], gap[:], log_shift[:, 0:1], 0.0, ALU.add, ALU.min)
-                nc.scalar.activation(accept[:, cols], ratio[:], ACT.Exp)
+            nc.vector.tensor_scalar(ratio[:], gap[:], log_shift[:, 0:1], 0.0, ALU.add, ALU.min)
+            nc.scalar.activation(accept[:, cols], ratio[:], ACT.Exp)
             if i != len(CHUNKS) - 2:
                 nc.sync.dma_start(out[0][:, stored:c0], accept[:, stored:c0])
                 stored = c0

@@ -69,7 +69,7 @@ def tile_attend_accept_srt_kernel(tc, qT, k_words, k_scales, ls, pd, offs, out):
             in_=q_bf[:].rearrange("p w j -> p (w j)"),
         )
         for r in range(4):
-            nc.scalar.dma_start(key_plane[r:P:32, :].bitcast(I32), listed_scales[ROW0 + ROW_STEP * r : ROW0 + 16 * ROW_STEP : 4 * ROW_STEP, :].bitcast(I32))
+            nc.sync.dma_start(key_plane[r:P:32, :].bitcast(I32), listed_scales[ROW0 + ROW_STEP * r : ROW0 + 16 * ROW_STEP : 4 * ROW_STEP, :].bitcast(I32))
         lse = sb.tile([P, 1], F32, name="lse", tag="q_bf", align_bytes=64)
         nc.sync.dma_start(lse[:], ls[0])
 

@@ -74,7 +74,8 @@ def tile_attend_accept_srt_kernel(tc, qT, k_words, k_scales, ls, pd, offs, out):
         nc.sync.dma_start(lse[:], ls[0])
 
         key_words = sb.tile([P, N], U32, name="key_words", align_bytes=64)
-        nc.vector.tensor_copy(key_words[:], word_pool[:].indirect(offsets[:]))
+        for h in range(2):
+            nc.vector.tensor_copy(key_words[:, h * 256 : (h + 1) * 256], word_pool[:].indirect(offsets[:, h * 16 : (h + 1) * 16]))
 
         accept = sb.tile([P, N], F32, name="accept")
         c0 = 0

@@ -16,9 +16,8 @@ P = 128
 PACK = 4
 D, T, N, NQ = 512, 4096, 512, 128
 CHUNKS = [128,128,128,128]
-DRAFT_PIECES = [(0, 256), (256, 512)]
+DRAFT_PIECES = [(0, 384), (384, 512)]
 ROW0, ROW_STEP = 32, 4
-FIRST = 256
 LOG2_SHIFT = 62
 FLOPS = 2 * D * NQ * N
 
@@ -42,11 +41,10 @@ def tile_attend_accept_srt_kernel(tc, qT, k_words, k_scales, ls, pd, offs, out):
         nc.sync.dma_start(q_raw[:], qT[0].rearrange("(p j) w -> p j w", j=PACK))
         nc.sync.dma_start(offsets[:], offs)
         words_hbm = k_words[0].rearrange("p n t -> p (n t)").bitcast(I32)
-        nc.sync.dma_start(word_pool[:, :FIRST].bitcast(I32), words_hbm[:, :FIRST])
+        nc.sync.dma_start(drafts[0][:], pd[0][:, slice(*DRAFT_PIECES[0])])
         nc.sync.dma_start(scale_pool[ROW0 : ROW0 + 16 * ROW_STEP : ROW_STEP, :].bitcast(I32), k_scales[0].bitcast(I32))
-        nc.sync.dma_start(word_pool[:, FIRST:].bitcast(I32), words_hbm[:, FIRST:])
-        for draft, (a, b) in zip(drafts, DRAFT_PIECES):
-            nc.sync.dma_start(draft[:], pd[0][:, a:b])
+        nc.sync.dma_start(word_pool[:].bitcast(I32), words_hbm)
+        nc.sync.dma_start(drafts[1][:], pd[0][:, slice(*DRAFT_PIECES[1])])
 
         one = sb.tile([P, 1], F32, name="one")
         nc.vector.memset(one[:], 1.0)
@@ -71,7 +69,8 @@ def tile_attend_accept_srt_kernel(tc, qT, k_words, k_scales, ls, pd, offs, out):
         for r in range(4):
             nc.sync.dma_start(key_plane[r:P:32, :].bitcast(I32), listed_scales[ROW0 + ROW_STEP * r : ROW0 + 16 * ROW_STEP : 4 * ROW_STEP, :].bitcast(I32))
         lse = sb.tile([P, 1], F32, name="lse", tag="q_bf", align_bytes=64)
-        nc.sync.dma_start(lse[:], ls[0])
+        for r in range(2):
+            nc.sync.dma_start(lse[r:P:2, :], ls[0][r:P:2, :])
 
         key_words = sb.tile([P, N], U32, name="key_words", align_bytes=64)
         for h in range(2):

@@ -16,7 +16,7 @@ P = 128
 PACK = 4
 D, T, N, NQ = 512, 4096, 512, 128
 CHUNKS = [128,128,128,128]
-DRAFT_PIECES = [(0, 384), (384, 512)]
+DRAFT_PIECES = [(0, 256), (256, 512)]
 ROW0, ROW_STEP = 32, 4
 LOG2_SHIFT = 62
 FLOPS = 2 * D * NQ * N
@@ -92,12 +92,15 @@ def tile_attend_accept_srt_kernel(tc, qT, k_words, k_scales, ls, pd, offs, out):
                 start=True,
                 stop=True,
             )
-            gap = sb.tile([P, width], F32, name="gap%d" % i)
+            if i < 2:
+                gap = sb.tile([P, width], F32, name="gap%d" % i)[:]
+            else:
+                gap = log_draft[:, (3 - i) * width : (4 - i) * width]
             nc.vector.scalar_tensor_tensor(
-                gap[:], acc[:], lse[:, 0:1], log_draft[:, cols], ALU.subtract, ALU.subtract
+                gap, acc[:], lse[:, 0:1], log_draft[:, cols], ALU.subtract, ALU.subtract
             )
             ratio = sb.tile([P, width], F32, name="ratio%d" % i)
-            nc.vector.tensor_scalar(ratio[:], gap[:], log_shift[:, 0:1], 0.0, ALU.add, ALU.min)
+            nc.vector.tensor_scalar(ratio[:], gap, log_shift[:, 0:1], 0.0, ALU.add, ALU.min)
             nc.scalar.activation(accept[:, cols], ratio[:], ACT.Exp)
             if i != len(CHUNKS) - 2:
                 nc.sync.dma_start(out[0][:, stored:c0], accept[:, stored:c0])

@@ -15,7 +15,8 @@ ACT = mybir.ActivationFunctionType
 P = 128
 PACK = 4
 D, T, N, NQ = 512, 4096, 512, 128
-CHUNKS = [128,128,128,128]
+CHUNK = 128
+STORE_ENDS = [128, 256, 512]
 DRAFT_PIECES = [(0, 256), (256, 512)]
 ROW0, ROW_STEP = 32, 4
 LOG2_SHIFT = 62
@@ -77,12 +78,10 @@ def tile_attend_accept_srt_kernel(tc, qT, k_words, k_scales, ls, pd, offs, out):
             nc.vector.tensor_copy(key_words[:, h * 256 : (h + 1) * 256], word_pool[:].indirect(offsets[:, h * 16 : (h + 1) * 16]))
 
         accept = sb.tile([P, N], F32, name="accept")
-        c0 = 0
-        stored = 0
-        for i, width in enumerate(CHUNKS):
-            cols = slice(c0, c0 + width)
-            c0 += width
-            acc = ps.tile([P, width], F32, name="acc%d" % i)
+        chunks = [slice(c0, c0 + CHUNK) for c0 in range(0, N, CHUNK)]
+        sums = []
+        for i, cols in enumerate(chunks):
+            acc = ps.tile([P, CHUNK], F32, name="acc%d" % i)
             nc.tensor.matmul_mx(
                 out=acc[:],
                 lhsT=q_words[:].bitcast(FP8X4),
@@ -92,16 +91,31 @@ def tile_attend_accept_srt_kernel(tc, qT, k_words, k_scales, ls, pd, offs, out):
                 start=True,
                 stop=True,
             )
-            if i < 2:
-                gap = sb.tile([P, width], F32, name="gap%d" % i)[:]
-            else:
-                gap = log_draft[:, (3 - i) * width : (4 - i) * width]
+            sums.append(acc)
+
+        first_gaps = sb.tile([P, N // 2], F32, name="first_gaps")
+        gaps = [first_gaps[:, cols] for cols in chunks[:2]] + [log_draft[:, cols] for cols in chunks[:2]]
+        ratio = sb.tile([P, N], F32, name="ratio")
+
+        def subtract(i):
             nc.vector.scalar_tensor_tensor(
-                gap, acc[:], lse[:, 0:1], log_draft[:, cols], ALU.subtract, ALU.subtract
+                gaps[i], sums[i][:], lse[:, 0:1], log_draft[:, chunks[i]], ALU.subtract, ALU.subtract
             )
-            ratio = sb.tile([P, width], F32, name="ratio%d" % i)
-            nc.vector.tensor_scalar(ratio[:], gap, log_shift[:, 0:1], 0.0, ALU.add, ALU.min)
-            nc.scalar.activation(accept[:, cols], ratio[:], ACT.Exp)
-            if i != len(CHUNKS) - 2:
-                nc.sync.dma_start(out[0][:, stored:c0], accept[:, stored:c0])
-                stored = c0
+
+        def cap(i):
+            nc.vector.tensor_scalar(ratio[:, chunks[i]], gaps[i], log_shift[:, 0:1], 0.0, ALU.add, ALU.min)
+
+        subtract(0)
+        subtract(1)
+        cap(0)
+        subtract(2)
+        subtract(3)
+        for i in range(1, len(chunks)):
+            cap(i)
+
+        stored = 0
+        for cols in chunks:
+            nc.scalar.activation(accept[:, cols], ratio[:, cols], ACT.Exp)
+            if cols.stop in STORE_ENDS:
+                nc.sync.dma_start(out[0][:, stored : cols.stop], accept[:, stored : cols.stop])
+                stored = cols.stop

@@ -17,7 +17,7 @@ PACK = 4
 D, T, N, NQ = 512, 4096, 512, 128
 CHUNK = 128
 STORE_ENDS = [128, 256, 512]
-DRAFT_PIECES = [(0, 256), (256, 512)]
+DRAFT_PIECES = [(0, 256), (256, 384), (384, 512)]
 ROW0, ROW_STEP = 32, 4
 LOG2_SHIFT = 62
 FLOPS = 2 * D * NQ * N
@@ -45,7 +45,8 @@ def tile_attend_accept_srt_kernel(tc, qT, k_words, k_scales, ls, pd, offs, out):
         nc.sync.dma_start(drafts[0][:], pd[0][:, slice(*DRAFT_PIECES[0])])
         nc.sync.dma_start(scale_pool[ROW0 : ROW0 + 16 * ROW_STEP : ROW_STEP, :].bitcast(I32), k_scales[0].bitcast(I32))
         nc.sync.dma_start(word_pool[:].bitcast(I32), words_hbm)
-        nc.sync.dma_start(drafts[1][:], pd[0][:, slice(*DRAFT_PIECES[1])])
+        for draft, (a, b) in zip(drafts[1:], DRAFT_PIECES[1:]):
+            nc.sync.dma_start(draft[:], pd[0][:, a:b])
 
         one = sb.tile([P, 1], F32, name="one")
         nc.vector.memset(one[:], 1.0)
@@ -70,8 +71,7 @@ def tile_attend_accept_srt_kernel(tc, qT, k_words, k_scales, ls, pd, offs, out):
         for r in range(4):
             nc.sync.dma_start(key_plane[r:P:32, :].bitcast(I32), listed_scales[ROW0 + ROW_STEP * r : ROW0 + 16 * ROW_STEP : 4 * ROW_STEP, :].bitcast(I32))
         lse = sb.tile([P, 1], F32, name="lse", tag="q_bf", align_bytes=64)
-        for r in range(2):
-            nc.sync.dma_start(lse[r:P:2, :], ls[0][r:P:2, :])
+        nc.sync.dma_start(lse[:], ls[0])
 
         key_words = sb.tile([P, N], U32, name="key_words", align_bytes=64)
         for h in range(2):

from contextlib import ExitStack

import concourse.mybir as mybir

F32 = mybir.dt.float32
BF16 = mybir.dt.bfloat16
I32 = mybir.dt.int32
U32 = mybir.dt.uint32
U16 = mybir.dt.uint16
U8 = mybir.dt.uint8
FP8X4 = mybir.dt.float8_e4m3fn_x4
ALU = mybir.AluOpType
ACT = mybir.ActivationFunctionType

P = 128
PACK = 4
D, T, N, NQ = 512, 4096, 512, 128
CHUNK = 128
STORE_ENDS = [128, 256, 512]
DRAFT_PIECES = [(0, 256), (256, 384), (384, 512)]
ROW0, ROW_STEP = 32, 4
LOG2_SHIFT = 62
FLOPS = 2 * D * NQ * N


def tile_attend_accept_srt_kernel(tc, qT, k_words, k_scales, ls, pd, offs, out):
    nc = tc.nc
    with ExitStack() as ctx:
        sb = ctx.enter_context(tc.tile_pool(name="sb", bufs=1))
        ps = ctx.enter_context(tc.psum_pool(name="ps", bufs=1))

        offsets = sb.tile([P, N // 16], U16, name="offsets")

        scale_pool = sb.tile([P, T], U8, name="scale_pool", align_bytes=64)
        nc.vector.memset(scale_pool[:].bitcast(I32), 0)
        key_plane = sb.tile([P, N], U8, name="key_plane", align_bytes=64)
        nc.vector.memset(key_plane[:].bitcast(I32), 0)

        drafts = [sb.tile([P, b - a], F32, name="draft%d" % a) for a, b in DRAFT_PIECES]
        q_raw = sb.tile([P, PACK, NQ], F32, name="q_raw")
        word_pool = sb.tile([P, T], U32, name="word_pool", align_bytes=64)
        nc.sync.dma_start(q_raw[:], qT[0].rearrange("(p j) w -> p j w", j=PACK))
        nc.sync.dma_start(offsets[:], offs)
        words_hbm = k_words[0].rearrange("p n t -> p (n t)").bitcast(I32)
        nc.sync.dma_start(drafts[0][:], pd[0][:, slice(*DRAFT_PIECES[0])])
        nc.sync.dma_start(scale_pool[ROW0 : ROW0 + 16 * ROW_STEP : ROW_STEP, :].bitcast(I32), k_scales[0].bitcast(I32))
        nc.sync.dma_start(word_pool[:].bitcast(I32), words_hbm)
        for draft, (a, b) in zip(drafts[1:], DRAFT_PIECES[1:]):
            nc.sync.dma_start(draft[:], pd[0][:, a:b])

        one = sb.tile([P, 1], F32, name="one")
        nc.vector.memset(one[:], 1.0)
        log_shift = sb.tile([P, 1], F32, name="log_shift")
        nc.scalar.activation(log_shift[:], one[:], ACT.Ln, scale=2.0**LOG2_SHIFT)
        log_draft = sb.tile([P, N], F32, name="log_draft")

        for draft, (a, b) in zip(drafts, DRAFT_PIECES):
            nc.scalar.activation(log_draft[:, a:b], draft[:], ACT.Ln, scale=2.0**LOG2_SHIFT)

        q_bf = sb.tile([P, NQ, PACK], BF16, name="q_bf", tag="q_bf", align_bytes=64)
        nc.vector.tensor_copy(q_bf[:], q_raw[:].rearrange("p j w -> p w j"))
        listed_scales = sb.tile([P, N], U8, name="listed_scales", align_bytes=64)
        nc.vector.tensor_copy(listed_scales[:], scale_pool[:].indirect(offsets[:]))
        q_words = sb.tile([P, NQ], U32, name="q_words", align_bytes=64)
        q_plane = sb.tile([P, NQ], U8, name="q_plane", align_bytes=64)
        nc.vector.quantize_mx(
            out=q_words[:].bitcast(FP8X4),
            scales=q_plane[:],
            in_=q_bf[:].rearrange("p w j -> p (w j)"),
        )
        for r in range(4):
            nc.sync.dma_start(key_plane[r:P:32, :].bitcast(I32), listed_scales[ROW0 + ROW_STEP * r : ROW0 + 16 * ROW_STEP : 4 * ROW_STEP, :].bitcast(I32))
        lse = sb.tile([P, 1], F32, name="lse", tag="q_bf", align_bytes=64)
        nc.sync.dma_start(lse[:], ls[0])

        key_words = sb.tile([P, N], U32, name="key_words", align_bytes=64)
        for h in range(2):
            nc.vector.tensor_copy(key_words[:, h * 256 : (h + 1) * 256], word_pool[:].indirect(offsets[:, h * 16 : (h + 1) * 16]))

        accept = sb.tile([P, N], F32, name="accept")
        chunks = [slice(c0, c0 + CHUNK) for c0 in range(0, N, CHUNK)]
        sums = []
        for i, cols in enumerate(chunks):
            acc = ps.tile([P, CHUNK], F32, name="acc%d" % i)
            nc.tensor.matmul_mx(
                out=acc[:],
                lhsT=q_words[:].bitcast(FP8X4),
                lhsT_scale=q_plane[:],
                rhs=key_words[:, cols].bitcast(FP8X4),
                rhs_scale=key_plane[:, cols],
                start=True,
                stop=True,
            )
            sums.append(acc)

        first_gaps = sb.tile([P, N // 2], F32, name="first_gaps")
        gaps = [first_gaps[:, cols] for cols in chunks[:2]] + [log_draft[:, cols] for cols in chunks[:2]]
        ratio = sb.tile([P, N], F32, name="ratio")

        def subtract(i):
            nc.vector.scalar_tensor_tensor(
                gaps[i], sums[i][:], lse[:, 0:1], log_draft[:, chunks[i]], ALU.subtract, ALU.subtract
            )

        def cap(i):
            nc.vector.tensor_scalar(ratio[:, chunks[i]], gaps[i], log_shift[:, 0:1], 0.0, ALU.add, ALU.min)

        subtract(0)
        subtract(1)
        cap(0)
        subtract(2)
        subtract(3)
        for i in range(1, len(chunks)):
            cap(i)

        stored = 0
        for cols in chunks:
            nc.scalar.activation(accept[:, cols], ratio[:, cols], ACT.Exp)
            if cols.stop in STORE_ENDS:
                nc.sync.dma_start(out[0][:, stored : cols.stop], accept[:, stored : cols.stop])
                stored = cols.stop
